import numpy as np
import ml_dtypes


def mxq(x, axis, fmt="e4m3"):
    dtype, down = {"e4m3": (ml_dtypes.float8_e4m3fn, 7), "e5m2": (ml_dtypes.float8_e5m2, 14)}[fmt]
    v = np.moveaxis(np.asarray(x, np.float32).astype(ml_dtypes.bfloat16).astype(np.float64), axis, -1)
    blocks = v.reshape(v.shape[:-1] + (-1, 32))
    amax = np.abs(blocks).max(-1, keepdims=True)
    byte = np.maximum(np.where(amax > 0, np.frexp(amax)[1] - 1 + 127, 0) - down, 1)
    scale = np.exp2(byte - 127.0)
    codes = (blocks / scale).astype(np.float32).astype(dtype).astype(np.float64)
    return np.moveaxis((codes * scale).reshape(v.shape), -1, axis)


WIDE = False


def mx_kscale(k):
    if not WIDE:
        return np.ones(k)
    levels = np.array([10, -10, 5, -5, 0])
    if k % 512:
        return np.exp2(np.random.permutation(np.resize(levels, k // 32))).repeat(32)
    a = np.empty((k // 512, 16))
    for p in range(k // 512):
        a[p, :8] = np.random.permutation(np.resize(levels, 8))
        for g in range(8):
            far = levels[np.abs(levels - a[p, g]) >= 10]
            a[p, g + 8] = far[np.random.randint(len(far))]
    return np.exp2(a.ravel()).repeat(32)


def f64(x):
    return np.asarray(x).astype(np.float64)


def striped8(idx):
    return np.asarray(idx).reshape(8, -1, 16).transpose(0, 2, 1).reshape(128, -1).astype(np.uint16)


def unstriped8(offs):
    return offs.reshape(8, 16, -1).transpose(0, 2, 1).reshape(8, -1).astype(np.int64)


def pick8(x, idx, run):
    r = np.arange(len(x))
    return x[r[:, None], idx[r % (8 * run) // run]]


E2M1 = np.array([0.0, 0.5, 1.0, 1.5, 2.0, 3.0, 4.0, 6.0, -0.0, -0.5, -1.0, -1.5, -2.0, -3.0, -4.0, -6.0])


def pack_weight(w, fmt):
    k, n = w.shape
    w = f64(np.asarray(w, np.float32).astype(ml_dtypes.bfloat16)).reshape(k // 32, 32, n)
    amax = np.abs(w).max(1)
    if fmt == "e4m3":
        byte = np.frexp(amax)[1] - 1 + 127 - 7
    else:
        mant, ex = np.frexp(amax / 6.0)
        byte = np.where(mant > 0.5, ex, ex - 1) + 127
    byte = np.clip(np.where(amax > 0, byte, 1), 1, 254)
    scaled = (w * np.exp2(127.0 - byte)[:, None, :]).reshape(k, n).astype(np.float32)
    by_word = np.ascontiguousarray(scaled.reshape(k // 512, 128, 4, n).transpose(0, 1, 3, 2))
    if fmt == "e4m3":
        words = by_word.astype(ml_dtypes.float8_e4m3fn).view(np.uint8)
    else:
        c = by_word.astype(ml_dtypes.float4_e2m1fn).view(np.uint8) & 0xF
        words = (c[..., 0::2] | (c[..., 1::2] << 4)).reshape(k // 512, 128, 2 * n)
    return np.ascontiguousarray(words), np.ascontiguousarray(byte.astype(np.uint8).reshape(k // 512, 16, n))


def unpack_weight(words, scales, fmt):
    g, _, n = scales.shape
    words = np.ascontiguousarray(words).reshape(g, 128, n, -1)
    if fmt == "e4m3":
        vals = words.view(ml_dtypes.float8_e4m3fn).astype(np.float64)
    else:
        nib = np.empty((g, 128, n, 4), np.uint8)
        nib[..., 0::2] = words & 0xF
        nib[..., 1::2] = words >> 4
        vals = E2M1[nib]
    vals = vals * np.repeat(np.exp2(scales.astype(np.float64) - 127.0), 8, axis=1)[..., None]
    return vals.transpose(0, 1, 3, 2).reshape(g * 512, n)


D, T, I, Q = 512, 1024, 512, 128


def setup_inputs():
    n = np.random.standard_normal
    idx = np.stack([np.random.permutation(T)[:I] for _ in range(8)])
    idx2 = np.stack([np.random.permutation(T)[:I] for _ in range(8)])
    idx4 = np.stack([np.random.permutation(T)[:I] for _ in range(8)])
    fd = mx_kscale(D)
    keysp = pack_weight(n((D, T)) / fd[:, None], "e4m3")
    return {
        "query": (n((D, Q)) * 0.9 / np.sqrt(D) * fd[:, None]).astype(np.float32),
        "query2": (n((D, Q)) * 0.9 / np.sqrt(D) * fd[:, None]).astype(np.float32),
        "keys_words": keysp[0],
        "keys_scales": keysp[1],
        "lam": (np.random.uniform(0.5, 1.3, (Q, 1))).astype(np.float32),
        "level": (np.random.uniform(0.05, 0.2, (Q, 1))).astype(np.float32),
        "old": (np.random.uniform(0.0, 2.0, (Q, T))).astype(np.float32),
        "gainm": (np.random.uniform(0.5, 1.5, (Q, I))).astype(np.float32),
        "offs": striped8(idx),
        "offs2": striped8(idx2),
        "offs4": striped8(idx4),
    }


def reference(query, query2, keys_words, keys_scales, lam, level, old, gainm, offs, offs2, offs4):
    idx = unstriped8(offs)
    idx2 = unstriped8(offs2)
    idx4 = unstriped8(offs4)
    keysu = unpack_weight(keys_words, keys_scales, "e4m3")
    queryq = mxq(f64(query), 0, "e4m3")
    a = queryq.T @ keysu
    query2q = mxq(f64(query2), 0, "e4m3")
    b = query2q.T @ keysu
    s = (np.maximum(pick8(a, idx, 16), pick8(b, idx2, 16)) - np.maximum(pick8(a, idx2, 16), pick8(b, idx, 16))) * f64(lam)
    p = np.exp(s - np.max(s, axis=1, keepdims=True))
    r = p / np.sum(p, axis=1, keepdims=True)
    w = np.maximum(r - np.max(r, axis=1, keepdims=True) * f64(level), 0.0)
    ws = w * f64(gainm) * 256.0
    wf = np.zeros((Q, T))
    wf[np.arange(Q)[:, None], idx4[np.arange(Q) % 128 // 16]] = ws
    y = f64(old) + wf
    return y

@@ -1,0 +1,164 @@
+from contextlib import ExitStack
+
+import concourse.mybir as mybir
+
+D, T, I, Q = 512, 1024, 512, 128
+P = 128
+PACK = 4
+FLOPS = 2 * 2 * D * T * Q
+
+F32 = mybir.dt.float32
+BF16 = mybir.dt.bfloat16
+I32 = mybir.dt.int32
+U32 = mybir.dt.uint32
+U16 = mybir.dt.uint16
+U8 = mybir.dt.uint8
+FP8X4 = mybir.dt.float8_e4m3fn_x4
+ALU = mybir.AluOpType
+ACT = mybir.ActivationFunctionType
+
+BANK = 512
+HALF = I // 2
+FIRST = 192
+PIECE = 256
+
+
+def tile_attend_exchanged_excess_moved_heads_kernel(
+    tc, query, query2, keys_words, keys_scales, lam, level, old, gainm, offs, offs2, offs4, out
+):
+    nc = tc.nc
+    with ExitStack() as ctx:
+        sb = ctx.enter_context(tc.tile_pool(name="sb", bufs=1))
+        ps = ctx.enter_context(tc.psum_pool(name="ps", bufs=1))
+
+        plane = sb.tile([P, T], U8, name="plane", align_bytes=64)
+        nc.gpsimd.memset(plane[:].bitcast(U32), 0)
+        wf = sb.tile([P, T], F32, name="wf")
+        nc.vector.memset(wf[:], 0.0)
+
+        raw = [sb.tile([P, PACK, Q], F32, name=f"raw{s}") for s in range(2)]
+        words = [sb.tile([P, BANK], U32, name=f"words{c}", align_bytes=64) for c in range(2)]
+        words_hbm = keys_words[0].rearrange("p n t -> p (n t)").bitcast(I32)
+
+        lam_t = sb.tile([P, 1], F32, name="lam_t")
+        level_t = sb.tile([P, 1], F32, name="level_t")
+        nc.gpsimd.dma_start(out=lam_t[:], in_=lam)
+        nc.gpsimd.dma_start(out=level_t[:], in_=level)
+
+        nc.sync.dma_start(out=raw[0][:], in_=query.rearrange("(p j) w -> p j w", j=PACK))
+        for g in range(4):
+            nc.sync.dma_start(
+                out=plane[32 * g : 32 * g + 4, :].bitcast(I32),
+                in_=keys_scales[0, 4 * g : 4 * g + 4, :].bitcast(I32),
+            )
+        nc.sync.dma_start(out=words[0][:].bitcast(I32), in_=words_hbm[:, 0:BANK])
+        nc.sync.dma_start(out=raw[1][:], in_=query2.rearrange("(p j) w -> p j w", j=PACK))
+        nc.sync.dma_start(out=words[1][:].bitcast(I32), in_=words_hbm[:, BANK:T])
+        l1 = sb.tile([P, I // 16], U16, name="l1")
+        l2 = sb.tile([P, I // 16], U16, name="l2")
+        l4 = sb.tile([P, I // 16], U16, name="l4")
+        nc.sync.dma_start(l1[:], offs)
+        nc.sync.dma_start(l2[:], offs2)
+        nc.sync.dma_start(l4[:], offs4)
+        gain_t = sb.tile([P, I], F32, name="gain_t")
+        old_t = sb.tile([P, T], F32, name="old_t")
+        nc.sync.dma_start(out=gain_t[:], in_=gainm)
+        nc.sync.dma_start(out=old_t[:], in_=old)
+
+        neg_level = sb.tile([P, 1], F32, name="neg_level")
+        nc.gpsimd.tensor_scalar(neg_level[:], level_t[:], -1.0, 0.0, ALU.mult, ALU.add)
+
+        grouped = [sb.tile([P, Q, PACK], BF16, name=f"grouped{s}", align_bytes=64) for s in range(2)]
+        codes = [sb.tile([P, Q], U32, name=f"codes{s}", align_bytes=64) for s in range(2)]
+        qscale = [sb.tile([P, Q], U8, name=f"qscale{s}", align_bytes=64) for s in range(2)]
+
+        def views(s):
+            return (
+                grouped[s][:].rearrange("p (c i) t -> p c t i", i=4),
+                raw[s][:].rearrange("p t (c i) -> p c t i", i=4),
+            )
+
+        def quantise(s):
+            nc.vector.quantize_mx(
+                out=codes[s][:].bitcast(FP8X4),
+                scales=qscale[s][:],
+                in_=grouped[s][:].rearrange("p w j -> p (w j)"),
+            )
+
+        dst, src = views(0)
+        nc.vector.tensor_copy(out=dst, in_=src)
+        quantise(0)
+        dst, src = views(1)
+        nc.vector.tensor_copy(out=dst, in_=src)
+        quantise(1)
+
+        score = [sb.tile([P, T], F32, name=f"score{s}") for s in range(2)]
+        for s in range(2):
+            for c in range(2):
+                cols = slice(c * BANK, (c + 1) * BANK)
+                acc = ps.tile([P, BANK], F32, name=f"acc{s}{c}")
+                nc.tensor.matmul_mx(
+                    out=acc[:],
+                    lhsT=codes[s][:].bitcast(FP8X4),
+                    lhsT_scale=qscale[s][:],
+                    rhs=words[c][:].bitcast(FP8X4),
+                    rhs_scale=plane[:, cols],
+                    start=True,
+                    stop=True,
+                )
+                if s == 0 and c == 0:
+                    nc.scalar.activation(score[s][:, cols], acc[:], ACT.Copy)
+                else:
+                    nc.vector.tensor_copy(out=score[s][:, cols], in_=acc[:])
+        a, b = score
+
+        def half(lst, h):
+            return lst[:, h * (HALF // 16) : (h + 1) * (HALF // 16)]
+
+        def fresh(name):
+            return [sb.tile([P, HALF], F32, name=f"{name}{h}") for h in range(2)]
+
+        a1, a2, b1, b2 = fresh("a1_"), fresh("a2_"), fresh("b1_"), fresh("b2_")
+        m1, m2, nd = fresh("m1_"), fresh("m2_"), fresh("nd_")
+        z = sb.tile([P, I], F32, name="z")
+        low = [sb.tile([P, 1], F32, name=f"low{h}") for h in range(2)]
+
+        for h in range(2):
+            nc.scalar.activation(a1[h][:], a[:].indirect(half(l1, h)), ACT.Copy)
+            nc.scalar.activation(a2[h][:], a[:].indirect(half(l2, h)), ACT.Copy)
+        nc.vector.tensor_copy(b2[0][:], b[:].indirect(half(l2, 0)))
+        nc.vector.tensor_copy(b1[0][:], b[:].indirect(half(l1, 0)))
+        nc.scalar.activation(b2[1][:], b[:].indirect(half(l2, 1)), ACT.Copy)
+        nc.scalar.activation(b1[1][:], b[:].indirect(half(l1, 1)), ACT.Copy)
+
+        nc.vector.tensor_tensor(m1[0][:], a1[0][:], b2[0][:], ALU.max)
+        nc.vector.tensor_tensor(m2[0][:], a2[0][:], b1[0][:], ALU.max)
+        nc.vector.tensor_tensor(m1[1][:], a1[1][:], b2[1][:], ALU.max)
+        nc.vector.tensor_tensor(nd[0][:], m2[0][:], m1[0][:], ALU.subtract)
+        nc.vector.tensor_tensor(m2[1][:], a2[1][:], b1[1][:], ALU.max)
+        nc.vector.tensor_scalar(z[:, 0:HALF], nd[0][:], lam_t[:], None, ALU.mult, ALU.min, accum_out=low[0][:])
+        nc.vector.tensor_tensor(nd[1][:], m2[1][:], m1[1][:], ALU.subtract)
+        nc.vector.tensor_scalar(z[:, HALF:I], nd[1][:], lam_t[:], low[0][:], ALU.mult, ALU.min, accum_out=low[1][:])
+
+        runs = (slice(0, FIRST), slice(FIRST, I))
+        p = [sb.tile([P, r.stop - r.start], F32, name=f"p{k}") for k, r in enumerate(runs)]
+        w = [sb.tile([P, r.stop - r.start], F32, name=f"w{k}") for k, r in enumerate(runs)]
+        part = [sb.tile([P, 1], F32, name=f"part{k}") for k in range(2)]
+        total = sb.tile([P, 1], F32, name="total")
+        inv = sb.tile([P, 1], F32, name="inv")
+        factor = sb.tile([P, 1], F32, name="factor")
+        for k, r in enumerate(runs):
+            nc.scalar.activation(p[k][:], z[:, r], ACT.Exp, bias=low[1][:], scale=-1.0, accum_out=part[k][:])
+        nc.vector.tensor_scalar(w[0][:], p[0][:], level_t[:], 0.0, ALU.subtract, ALU.max)
+        nc.scalar.activation(total[:], part[1][:], ACT.Identity, bias=part[0][:], scale=1.0)
+        nc.scalar.activation(w[1][:], p[1][:], ACT.Relu, bias=neg_level[:], scale=1.0)
+        nc.vector.tensor_tensor(wf[:].indirect(l4[:, 0 : FIRST // 16]), w[0][:], gain_t[:, runs[0]], ALU.mult)
+        nc.vector.reciprocal(inv[:], total[:])
+        nc.scalar.activation(factor[:], inv[:], ACT.Copy, scale=256.0)
+        nc.vector.tensor_tensor(wf[:].indirect(l4[:, FIRST // 16 : I // 16]), w[1][:], gain_t[:, runs[1]], ALU.mult)
+
+        for c in range(T // PIECE):
+            cols = slice(c * PIECE, (c + 1) * PIECE)
+            res = sb.tile([P, PIECE], F32, name=f"res{c}")
+            nc.vector.scalar_tensor_tensor(res[:], wf[:, cols], factor[:], old_t[:, cols], ALU.mult, ALU.add)
+            nc.sync.dma_start(out=out[:, cols], in_=res[:])

@@ -19,8 +19,9 @@ ACT = mybir.ActivationFunctionType
 
 BANK = 512
 HALF = I // 2
-FIRST = 192
-PIECE = 256
+FIRST = 128
+PIECES = (128, 256, 256, 256, 128)
+CHUNKS = ((512, 256, 128, 128), (256, 256, 256, 256))
 
 
 def tile_attend_exchanged_excess_moved_heads_kernel(
@@ -32,7 +33,7 @@ def tile_attend_exchanged_excess_moved_heads_kernel(
         ps = ctx.enter_context(tc.psum_pool(name="ps", bufs=1))
 
         plane = sb.tile([P, T], U8, name="plane", align_bytes=64)
-        nc.gpsimd.memset(plane[:].bitcast(U32), 0)
+        nc.vector.memset(plane[:].bitcast(U32), 0)
         wf = sb.tile([P, T], F32, name="wf")
         nc.vector.memset(wf[:], 0.0)
 
@@ -47,7 +48,7 @@ def tile_attend_exchanged_excess_moved_heads_kernel(
 
         nc.sync.dma_start(out=raw[0][:], in_=query.rearrange("(p j) w -> p j w", j=PACK))
         for g in range(4):
-            nc.sync.dma_start(
+            (nc.sync if g < 2 else nc.scalar).dma_start(
                 out=plane[32 * g : 32 * g + 4, :].bitcast(I32),
                 in_=keys_scales[0, 4 * g : 4 * g + 4, :].bitcast(I32),
             )
@@ -94,22 +95,25 @@ def tile_attend_exchanged_excess_moved_heads_kernel(
 
         score = [sb.tile([P, T], F32, name=f"score{s}") for s in range(2)]
         for s in range(2):
-            for c in range(2):
-                cols = slice(c * BANK, (c + 1) * BANK)
-                acc = ps.tile([P, BANK], F32, name=f"acc{s}{c}")
+            t0 = 0
+            for k, width in enumerate(CHUNKS[s]):
+                cols = slice(t0, t0 + width)
+                c, w0 = divmod(t0, BANK)
+                acc = ps.tile([P, width], F32, name=f"acc{s}{k}", tag="acc", bufs=8)
                 nc.tensor.matmul_mx(
                     out=acc[:],
                     lhsT=codes[s][:].bitcast(FP8X4),
                     lhsT_scale=qscale[s][:],
-                    rhs=words[c][:].bitcast(FP8X4),
+                    rhs=words[c][:, w0 : w0 + width].bitcast(FP8X4),
                     rhs_scale=plane[:, cols],
                     start=True,
                     stop=True,
                 )
-                if s == 0 and c == 0:
+                if s == 0 and k % 2 == 0:
                     nc.scalar.activation(score[s][:, cols], acc[:], ACT.Copy)
                 else:
                     nc.vector.tensor_copy(out=score[s][:, cols], in_=acc[:])
+                t0 = t0 + width
         a, b = score
 
         def half(lst, h):
@@ -131,13 +135,19 @@ def tile_attend_exchanged_excess_moved_heads_kernel(
         nc.scalar.activation(b2[1][:], b[:].indirect(half(l2, 1)), ACT.Copy)
         nc.scalar.activation(b1[1][:], b[:].indirect(half(l1, 1)), ACT.Copy)
 
+        quarters = (slice(0, HALF // 2), slice(HALF // 2, HALF))
+
+        def contrast(h):
+            for r in quarters:
+                nc.vector.tensor_tensor(m2[h][:, r], a2[h][:, r], b1[h][:, r], ALU.max)
+            for r in quarters:
+                nc.vector.tensor_tensor(nd[h][:, r], m2[h][:, r], m1[h][:, r], ALU.subtract)
+
         nc.vector.tensor_tensor(m1[0][:], a1[0][:], b2[0][:], ALU.max)
-        nc.vector.tensor_tensor(m2[0][:], a2[0][:], b1[0][:], ALU.max)
+        contrast(0)
         nc.vector.tensor_tensor(m1[1][:], a1[1][:], b2[1][:], ALU.max)
-        nc.vector.tensor_tensor(nd[0][:], m2[0][:], m1[0][:], ALU.subtract)
-        nc.vector.tensor_tensor(m2[1][:], a2[1][:], b1[1][:], ALU.max)
         nc.vector.tensor_scalar(z[:, 0:HALF], nd[0][:], lam_t[:], None, ALU.mult, ALU.min, accum_out=low[0][:])
-        nc.vector.tensor_tensor(nd[1][:], m2[1][:], m1[1][:], ALU.subtract)
+        contrast(1)
         nc.vector.tensor_scalar(z[:, HALF:I], nd[1][:], lam_t[:], low[0][:], ALU.mult, ALU.min, accum_out=low[1][:])
 
         runs = (slice(0, FIRST), slice(FIRST, I))
@@ -157,8 +167,10 @@ def tile_attend_exchanged_excess_moved_heads_kernel(
         nc.scalar.activation(factor[:], inv[:], ACT.Copy, scale=256.0)
         nc.vector.tensor_tensor(wf[:].indirect(l4[:, FIRST // 16 : I // 16]), w[1][:], gain_t[:, runs[1]], ALU.mult)
 
-        for c in range(T // PIECE):
-            cols = slice(c * PIECE, (c + 1) * PIECE)
-            res = sb.tile([P, PIECE], F32, name=f"res{c}")
+        t0 = 0
+        for c, width in enumerate(PIECES):
+            cols = slice(t0, t0 + width)
+            res = sb.tile([P, width], F32, name=f"res{c}")
             nc.vector.scalar_tensor_tensor(res[:], wf[:, cols], factor[:], old_t[:, cols], ALU.mult, ALU.add)
             nc.sync.dma_start(out=out[:, cols], in_=res[:])
+            t0 = t0 + width

@@ -43,8 +43,6 @@ def tile_attend_exchanged_excess_moved_heads_kernel(
 
         lam_t = sb.tile([P, 1], F32, name="lam_t")
         level_t = sb.tile([P, 1], F32, name="level_t")
-        nc.gpsimd.dma_start(out=lam_t[:], in_=lam)
-        nc.gpsimd.dma_start(out=level_t[:], in_=level)
 
         nc.sync.dma_start(out=raw[0][:], in_=query.rearrange("(p j) w -> p j w", j=PACK))
         for g in range(4):
@@ -60,14 +58,13 @@ def tile_attend_exchanged_excess_moved_heads_kernel(
         l4 = sb.tile([P, I // 16], U16, name="l4")
         nc.sync.dma_start(l1[:], offs)
         nc.sync.dma_start(l2[:], offs2)
+        nc.sync.dma_start(out=lam_t[:], in_=lam)
+        nc.sync.dma_start(out=level_t[:], in_=level)
         nc.sync.dma_start(l4[:], offs4)
         gain_t = sb.tile([P, I], F32, name="gain_t")
         old_t = sb.tile([P, T], F32, name="old_t")
         nc.sync.dma_start(out=gain_t[:], in_=gainm)
         nc.sync.dma_start(out=old_t[:], in_=old)
-
-        neg_level = sb.tile([P, 1], F32, name="neg_level")
-        nc.gpsimd.tensor_scalar(neg_level[:], level_t[:], -1.0, 0.0, ALU.mult, ALU.add)
 
         grouped = [sb.tile([P, Q, PACK], BF16, name=f"grouped{s}", align_bytes=64) for s in range(2)]
         codes = [sb.tile([P, Q], U32, name=f"codes{s}", align_bytes=64) for s in range(2)]
@@ -134,6 +131,9 @@ def tile_attend_exchanged_excess_moved_heads_kernel(
         nc.vector.tensor_copy(b1[0][:], b[:].indirect(half(l1, 0)))
         nc.scalar.activation(b2[1][:], b[:].indirect(half(l2, 1)), ACT.Copy)
         nc.scalar.activation(b1[1][:], b[:].indirect(half(l1, 1)), ACT.Copy)
+
+        neg_level = sb.tile([P, 1], F32, name="neg_level")
+        nc.scalar.activation(neg_level[:], level_t[:], ACT.Copy, scale=-1.0)
 
         quarters = (slice(0, HALF // 2), slice(HALF // 2, HALF))
 

from contextlib import ExitStack

import concourse.mybir as mybir

D, T, I, Q = 512, 1024, 512, 128
P = 128
PACK = 4
FLOPS = 2 * 2 * D * T * Q

F32 = mybir.dt.float32
BF16 = mybir.dt.bfloat16
I32 = mybir.dt.int32
U32 = mybir.dt.uint32
U16 = mybir.dt.uint16
U8 = mybir.dt.uint8
FP8X4 = mybir.dt.float8_e4m3fn_x4
ALU = mybir.AluOpType
ACT = mybir.ActivationFunctionType

BANK = 512
HALF = I // 2
FIRST = 128
PIECES = (128, 256, 256, 256, 128)
CHUNKS = ((512, 256, 128, 128), (256, 256, 256, 256))


def tile_attend_exchanged_excess_moved_heads_kernel(
    tc, query, query2, keys_words, keys_scales, lam, level, old, gainm, offs, offs2, offs4, out
):
    nc = tc.nc
    with ExitStack() as ctx:
        sb = ctx.enter_context(tc.tile_pool(name="sb", bufs=1))
        ps = ctx.enter_context(tc.psum_pool(name="ps", bufs=1))

        plane = sb.tile([P, T], U8, name="plane", align_bytes=64)
        nc.vector.memset(plane[:].bitcast(U32), 0)
        wf = sb.tile([P, T], F32, name="wf")
        nc.vector.memset(wf[:], 0.0)

        raw = [sb.tile([P, PACK, Q], F32, name=f"raw{s}") for s in range(2)]
        words = [sb.tile([P, BANK], U32, name=f"words{c}", align_bytes=64) for c in range(2)]
        words_hbm = keys_words[0].rearrange("p n t -> p (n t)").bitcast(I32)

        lam_t = sb.tile([P, 1], F32, name="lam_t")
        level_t = sb.tile([P, 1], F32, name="level_t")

        nc.sync.dma_start(out=raw[0][:], in_=query.rearrange("(p j) w -> p j w", j=PACK))
        for g in range(4):
            (nc.sync if g < 2 else nc.scalar).dma_start(
                out=plane[32 * g : 32 * g + 4, :].bitcast(I32),
                in_=keys_scales[0, 4 * g : 4 * g + 4, :].bitcast(I32),
            )
        nc.sync.dma_start(out=words[0][:].bitcast(I32), in_=words_hbm[:, 0:BANK])
        nc.sync.dma_start(out=raw[1][:], in_=query2.rearrange("(p j) w -> p j w", j=PACK))
        nc.sync.dma_start(out=words[1][:].bitcast(I32), in_=words_hbm[:, BANK:T])
        l1 = sb.tile([P, I // 16], U16, name="l1")
        l2 = sb.tile([P, I // 16], U16, name="l2")
        l4 = sb.tile([P, I // 16], U16, name="l4")
        nc.sync.dma_start(l1[:], offs)
        nc.sync.dma_start(l2[:], offs2)
        nc.sync.dma_start(out=lam_t[:], in_=lam)
        nc.sync.dma_start(out=level_t[:], in_=level)
        nc.sync.dma_start(l4[:], offs4)
        gain_t = sb.tile([P, I], F32, name="gain_t")
        old_t = sb.tile([P, T], F32, name="old_t")
        nc.sync.dma_start(out=gain_t[:], in_=gainm)
        nc.sync.dma_start(out=old_t[:], in_=old)

        grouped = [sb.tile([P, Q, PACK], BF16, name=f"grouped{s}", align_bytes=64) for s in range(2)]
        codes = [sb.tile([P, Q], U32, name=f"codes{s}", align_bytes=64) for s in range(2)]
        qscale = [sb.tile([P, Q], U8, name=f"qscale{s}", align_bytes=64) for s in range(2)]

        def views(s):
            return (
                grouped[s][:].rearrange("p (c i) t -> p c t i", i=4),
                raw[s][:].rearrange("p t (c i) -> p c t i", i=4),
            )

        def quantise(s):
            nc.vector.quantize_mx(
                out=codes[s][:].bitcast(FP8X4),
                scales=qscale[s][:],
                in_=grouped[s][:].rearrange("p w j -> p (w j)"),
            )

        dst, src = views(0)
        nc.vector.tensor_copy(out=dst, in_=src)
        quantise(0)
        dst, src = views(1)
        nc.vector.tensor_copy(out=dst, in_=src)
        quantise(1)

        score = [sb.tile([P, T], F32, name=f"score{s}") for s in range(2)]
        for s in range(2):
            t0 = 0
            for k, width in enumerate(CHUNKS[s]):
                cols = slice(t0, t0 + width)
                c, w0 = divmod(t0, BANK)
                acc = ps.tile([P, width], F32, name=f"acc{s}{k}", tag="acc", bufs=8)
                nc.tensor.matmul_mx(
                    out=acc[:],
                    lhsT=codes[s][:].bitcast(FP8X4),
                    lhsT_scale=qscale[s][:],
                    rhs=words[c][:, w0 : w0 + width].bitcast(FP8X4),
                    rhs_scale=plane[:, cols],
                    start=True,
                    stop=True,
                )
                if s == 0 and k % 2 == 0:
                    nc.scalar.activation(score[s][:, cols], acc[:], ACT.Copy)
                else:
                    nc.vector.tensor_copy(out=score[s][:, cols], in_=acc[:])
                t0 = t0 + width
        a, b = score

        def half(lst, h):
            return lst[:, h * (HALF // 16) : (h + 1) * (HALF // 16)]

        def fresh(name):
            return [sb.tile([P, HALF], F32, name=f"{name}{h}") for h in range(2)]

        a1, a2, b1, b2 = fresh("a1_"), fresh("a2_"), fresh("b1_"), fresh("b2_")
        m1, m2, nd = fresh("m1_"), fresh("m2_"), fresh("nd_")
        z = sb.tile([P, I], F32, name="z")
        low = [sb.tile([P, 1], F32, name=f"low{h}") for h in range(2)]

        for h in range(2):
            nc.scalar.activation(a1[h][:], a[:].indirect(half(l1, h)), ACT.Copy)
            nc.scalar.activation(a2[h][:], a[:].indirect(half(l2, h)), ACT.Copy)
        nc.vector.tensor_copy(b2[0][:], b[:].indirect(half(l2, 0)))
        nc.vector.tensor_copy(b1[0][:], b[:].indirect(half(l1, 0)))
        nc.scalar.activation(b2[1][:], b[:].indirect(half(l2, 1)), ACT.Copy)
        nc.scalar.activation(b1[1][:], b[:].indirect(half(l1, 1)), ACT.Copy)

        neg_level = sb.tile([P, 1], F32, name="neg_level")
        nc.scalar.activation(neg_level[:], level_t[:], ACT.Copy, scale=-1.0)

        quarters = (slice(0, HALF // 2), slice(HALF // 2, HALF))

        def contrast(h):
            for r in quarters:
                nc.vector.tensor_tensor(m2[h][:, r], a2[h][:, r], b1[h][:, r], ALU.max)
            for r in quarters:
                nc.vector.tensor_tensor(nd[h][:, r], m2[h][:, r], m1[h][:, r], ALU.subtract)

        nc.vector.tensor_tensor(m1[0][:], a1[0][:], b2[0][:], ALU.max)
        contrast(0)
        nc.vector.tensor_tensor(m1[1][:], a1[1][:], b2[1][:], ALU.max)
        nc.vector.tensor_scalar(z[:, 0:HALF], nd[0][:], lam_t[:], None, ALU.mult, ALU.min, accum_out=low[0][:])
        contrast(1)
        nc.vector.tensor_scalar(z[:, HALF:I], nd[1][:], lam_t[:], low[0][:], ALU.mult, ALU.min, accum_out=low[1][:])

        runs = (slice(0, FIRST), slice(FIRST, I))
        p = [sb.tile([P, r.stop - r.start], F32, name=f"p{k}") for k, r in enumerate(runs)]
        w = [sb.tile([P, r.stop - r.start], F32, name=f"w{k}") for k, r in enumerate(runs)]
        part = [sb.tile([P, 1], F32, name=f"part{k}") for k in range(2)]
        total = sb.tile([P, 1], F32, name="total")
        inv = sb.tile([P, 1], F32, name="inv")
        factor = sb.tile([P, 1], F32, name="factor")
        for k, r in enumerate(runs):
            nc.scalar.activation(p[k][:], z[:, r], ACT.Exp, bias=low[1][:], scale=-1.0, accum_out=part[k][:])
        nc.vector.tensor_scalar(w[0][:], p[0][:], level_t[:], 0.0, ALU.subtract, ALU.max)
        nc.scalar.activation(total[:], part[1][:], ACT.Identity, bias=part[0][:], scale=1.0)
        nc.scalar.activation(w[1][:], p[1][:], ACT.Relu, bias=neg_level[:], scale=1.0)
        nc.vector.tensor_tensor(wf[:].indirect(l4[:, 0 : FIRST // 16]), w[0][:], gain_t[:, runs[0]], ALU.mult)
        nc.vector.reciprocal(inv[:], total[:])
        nc.scalar.activation(factor[:], inv[:], ACT.Copy, scale=256.0)
        nc.vector.tensor_tensor(wf[:].indirect(l4[:, FIRST // 16 : I // 16]), w[1][:], gain_t[:, runs[1]], ALU.mult)

        t0 = 0
        for c, width in enumerate(PIECES):
            cols = slice(t0, t0 + width)
            res = sb.tile([P, width], F32, name=f"res{c}")
            nc.vector.scalar_tensor_tensor(res[:], wf[:, cols], factor[:], old_t[:, cols], ALU.mult, ALU.add)
            nc.sync.dma_start(out=out[:, cols], in_=res[:])
            t0 = t0 + width
